import numpy as np
import ml_dtypes


def mxq(x, axis, fmt="e4m3"):
    dtype, down = {"e4m3": (ml_dtypes.float8_e4m3fn, 7), "e5m2": (ml_dtypes.float8_e5m2, 14)}[fmt]
    v = np.moveaxis(np.asarray(x, np.float32).astype(ml_dtypes.bfloat16).astype(np.float64), axis, -1)
    blocks = v.reshape(v.shape[:-1] + (-1, 32))
    amax = np.abs(blocks).max(-1, keepdims=True)
    byte = np.maximum(np.where(amax > 0, np.frexp(amax)[1] - 1 + 127, 0) - down, 1)
    scale = np.exp2(byte - 127.0)
    codes = (blocks / scale).astype(np.float32).astype(dtype).astype(np.float64)
    return np.moveaxis((codes * scale).reshape(v.shape), -1, axis)


WIDE = False


def mx_kscale(k, group=512):
    if not WIDE:
        return np.ones(k)
    levels = np.array([10, -10, 5, -5, 0])
    if group != 512:
        return np.exp2(np.random.permutation(np.resize(levels, k // group))).repeat(group)
    if k % 512:
        return np.exp2(np.random.permutation(np.resize(levels, k // 32))).repeat(32)
    a = np.empty((k // 512, 16))
    for p in range(k // 512):
        a[p, :8] = np.random.permutation(np.resize(levels, 8))
        for g in range(8):
            far = levels[np.abs(levels - a[p, g]) >= 10]
            a[p, g + 8] = far[np.random.randint(len(far))]
    return np.exp2(a.ravel()).repeat(32)


def f64(x):
    return np.asarray(x).astype(np.float64)


def striped(idx):
    return np.tile(np.asarray(idx).reshape(-1, 16).T, (8, 1)).astype(np.uint16)


def unstriped(offs):
    return offs[:16].T.reshape(-1).astype(np.int64)


H, KV, D, NQ, N = 4, 4, 128, 512, 512


def setup_inputs():
    n = np.random.standard_normal
    s = mx_kscale(D, 0)[:, None]
    u = mx_kscale(N)
    t = np.random.uniform(0.5, 2.0, N) * u
    v = n((KV, N, 128))
    v[:, :, 127] = 1.0
    return {
        "qT": (n((H, D, NQ)) * s * (0.70 / np.sqrt(D))).astype(np.float32),
        "kT": (n((KV, D, N)) / s).astype(np.float32),
        "t": t.reshape(N, 1).astype(np.float32),
        "v": (v / t[:, None]).astype(np.float32),
        "og": n((H, NQ, 128)).astype(np.float32),
    }


def reference(qT, kT, t, v, og):
    a = mxq(f64(kT), 1, "e4m3").transpose(0, 2, 1) @ mxq(f64(qT), 1, "e4m3")
    p = np.exp(a)
    w = p * f64(t)
    y = mxq(w, 1, "e4m3").transpose(0, 2, 1) @ mxq(f64(v), 1, "e4m3")
    y = y / (y[:, :, 127:128])
    y = y / (1.0 + np.exp(-f64(og)))
    return y

@@ -1,0 +1,219 @@
+from contextlib import ExitStack
+
+import concourse.mybir as mybir
+
+H, D, NQ, N = 4, 128, 512, 512
+FLOPS = 2 * 2 * H * NQ * N * D
+
+F32 = mybir.dt.float32
+BF16 = mybir.dt.bfloat16
+U32 = mybir.dt.uint32
+U8 = mybir.dt.uint8
+FP8X4 = mybir.dt.float8_e4m3fn_x4
+ALU = mybir.AluOpType
+ACT = mybir.ActivationFunctionType
+
+P = 128
+PACK = 4
+ROWS = 32
+T = 128
+LN_LOW = 2.0 ** -63
+LN_HIGH = 2.0 ** 64
+Q_VECTOR = 84
+BANKS = (2, 2, 1, 2)
+
+
+def tile_rows_gate_kernel(tc, qT, kT, t, v, og, out):
+    nc = tc.nc
+    with ExitStack() as ctx:
+        sb = ctx.enter_context(tc.tile_pool(name="sb", bufs=1))
+        ps = ctx.enter_context(tc.psum_pool(name="ps", bufs=1))
+        ctx.enter_context(tc.manual_schedule())
+
+        def sbuf(name, width, dtype):
+            return sb.tile([P, width], dtype, name=name, align_bytes=64)
+
+        t_raw = sbuf("t_raw", PACK, F32)
+        og_first = sbuf("og_first", T, F32)
+        og_rest = sbuf("og_rest", 3 * T, F32)
+        k_raw = sbuf("k_raw", PACK * N, F32)
+        q_raw = sbuf("q_raw", PACK * NQ, F32)
+        v_raw = [sbuf("v_raw%d" % h, PACK * T, F32) for h in range(H)]
+        og_raw = [None] + [sbuf("og_raw%d" % h, PACK * T, F32) for h in range(1, H)]
+        og_rows = og.rearrange("h (m c) e -> h m (c e)", c=PACK)
+        out_rows = out.rearrange("h (m c) e -> h m (c e)", c=PACK)
+
+        nc.sync.dma_start(out=t_raw[:], in_=t.rearrange("(p j) o -> p (j o)", j=PACK))
+        nc.sync.dma_start(out=k_raw[:], in_=kT.rearrange("h (p j) n -> (h p) (j n)", j=PACK))
+        nc.scalar.dma_start(out=og_first[:], in_=og_rows[0, :, 0:T])
+        nc.sync.dma_start(out=q_raw[:], in_=qT.rearrange("h (p j) n -> (h p) (j n)", j=PACK))
+        for h in range(H):
+            nc.sync.dma_start(out=v_raw[h][:], in_=v[h].rearrange("(p j) e -> p (j e)", j=PACK))
+        nc.sync.dma_start(out=og_rest[:], in_=og_rows[0, :, T:])
+        for h in range(1, H):
+            nc.sync.dma_start(out=og_raw[h][:], in_=og_rows[h])
+
+        t_abs = sbuf("t_abs", PACK, F32)
+        t_sign = sbuf("t_sign", PACK, F32)
+        t_step = sbuf("t_step", PACK, F32)
+        t_inv = sbuf("t_inv", PACK, F32)
+        t_parts = sbuf("t_parts", 2 * PACK, F32)
+        ln_parts = sbuf("ln_parts", 2 * PACK, F32)
+        ln_t = sbuf("ln_t", PACK, F32)
+        nc.vector.scalar_tensor_tensor(out=t_abs[:], in0=t_raw[:], scalar=-1.0, in1=t_raw[:], op0=ALU.mult, op1=ALU.max)
+        nc.vector.tensor_scalar(out=t_step[:], in0=t_raw[:], scalar1=0.0, scalar2=2.0, op0=ALU.is_ge, op1=ALU.mult)
+        nc.vector.tensor_scalar(out=t_parts[:, 0:PACK], in0=t_abs[:], scalar1=LN_LOW, scalar2=LN_HIGH, op0=ALU.max, op1=ALU.min)
+        nc.vector.tensor_scalar(out=t_sign[:], in0=t_step[:], scalar1=-1.0, scalar2=None, op0=ALU.add)
+        nc.vector.reciprocal(out=t_inv[:], in_=t_parts[:, 0:PACK])
+        nc.vector.tensor_tensor(out=t_parts[:, PACK:], in0=t_abs[:], in1=t_inv[:], op=ALU.mult)
+        nc.scalar.activation(out=ln_parts[:], in_=t_parts[:], func=ACT.Ln)
+
+        gate = [sbuf("gate%d" % h, PACK * T, F32) for h in range(H)]
+        tanh_g = [sbuf("tanh_g%d" % h, PACK * T, F32) for h in range(H)]
+        nc.scalar.activation(out=tanh_g[0][:, 0:T], in_=og_first[:], func=ACT.Tanh, scale=0.5)
+
+        k_bf = sbuf("k_bf", PACK * N, BF16)
+        q_bf = sbuf("q_bf", PACK * NQ, BF16)
+        k_codes = sbuf("k_codes", N, U32)
+        k_scales = sbuf("k_scales", N, U8)
+        q_codes = [sbuf("q_codes%d" % u, NQ // 2, U32) for u in range(2)]
+        q_scales = [sbuf("q_scales%d" % u, NQ // 2, U8) for u in range(2)]
+
+        def dealt(bf, raw):
+            return (bf[:].rearrange("p (c m j) -> p m j c", c=PACK, j=PACK),
+                    raw[:].rearrange("p (j m c) -> p m j c", c=PACK, j=PACK))
+
+        k_dst, k_src = dealt(k_bf, k_raw)
+        nc.vector.tensor_copy(out=k_dst, in_=k_src)
+        nc.vector.tensor_tensor(out=ln_t[:], in0=ln_parts[:, 0:PACK], in1=ln_parts[:, PACK:], op=ALU.add)
+        nc.vector.quantize_mx(out=k_codes[:].bitcast(FP8X4), scales=k_scales[:], in_=k_bf[:])
+        q_dst, q_src = dealt(q_bf, q_raw)
+        nc.vector.tensor_copy(out=q_dst[:, 0:Q_VECTOR], in_=q_src[:, 0:Q_VECTOR])
+        nc.scalar.copy(out=q_dst[:, Q_VECTOR:], in_=q_src[:, Q_VECTOR:])
+        for u in range(2):
+            nc.vector.quantize_mx(out=q_codes[u][:].bitcast(FP8X4), scales=q_scales[u][:],
+                                  in_=q_bf[:, u * 2 * NQ:(u + 1) * 2 * NQ])
+
+        v_bf = [sbuf("v_bf%d" % g, 2 * PACK * T, BF16) for g in range(2)]
+        v_codes = [sbuf("v_codes%d" % g, 2 * T, U32) for g in range(2)]
+        v_scales = [sbuf("v_scales%d" % g, 2 * T, U8) for g in range(2)]
+        sign_b = t_sign[:, 0:PACK].unsqueeze(1).unsqueeze(3).to_broadcast([P, T // 4, PACK, 4])
+        for h in range(H):
+            dst = v_bf[h // 2][:, (h % 2) * PACK * T:(h % 2 + 1) * PACK * T]
+            nc.vector.tensor_tensor(out=dst.rearrange("p (c i j) -> p c j i", i=4, j=PACK),
+                                    in0=v_raw[h][:].rearrange("p (j c i) -> p c j i", i=4, j=PACK),
+                                    in1=sign_b, op=ALU.mult)
+        for g in range(2):
+            nc.vector.quantize_mx(out=v_codes[g][:].bitcast(FP8X4), scales=v_scales[g][:], in_=v_bf[g][:])
+
+        banks = [[ps.tile([P, NQ], F32, name="score%d_%d" % (h, b)) for b in range(BANKS[h])] for h in range(H)]
+        y_bank = ps.tile([P, PACK * T], F32, name="y_bank")
+        w_rows = [sbuf("w_rows%d" % h, PACK * NQ, BF16) for h in range(H)]
+        w_bf = [[sbuf("w_bf%d_%d" % (h, u), 2 * NQ, BF16) for u in range(2)] for h in range(H)]
+        w_codes = [[sbuf("w_codes%d_%d" % (h, u), NQ // 2, U32) for u in range(2)] for h in range(H)]
+        w_scales = [[sbuf("w_scales%d_%d" % (h, u), NQ // 2, U8) for u in range(2)] for h in range(H)]
+        rec = [sbuf("rec%d" % h, PACK, F32) for h in range(H)]
+        res = [[sbuf("res%d_%d" % (h, u), 2 * T, F32) for u in range(2)] for h in range(H)]
+
+        def scores(h, r):
+            bank = banks[h][r % BANKS[h]]
+            rows = slice(ROWS * h, ROWS * (h + 1))
+            keys = slice(T * r, T * (r + 1))
+            for c in range(PACK):
+                cols = slice(T * (c % 2), T * (c % 2 + 1))
+                nc.tensor.matmul_mx(out=bank[:, T * c:T * (c + 1)],
+                                    lhsT=k_codes[rows, keys].bitcast(FP8X4), lhsT_scale=k_scales[rows, keys],
+                                    rhs=q_codes[c // 2][rows, cols].bitcast(FP8X4), rhs_scale=q_scales[c // 2][rows, cols],
+                                    start=True, stop=True)
+
+        def weights(h, r):
+            nc.scalar.activation(out=w_rows[h][:, NQ * r:NQ * (r + 1)], in_=banks[h][r % BANKS[h]][:],
+                                 func=ACT.Exp, bias=ln_t[:, r:r + 1])
+
+        def tanh(h):
+            if h == 0:
+                nc.scalar.activation(out=tanh_g[0][:, T:], in_=og_rest[:], func=ACT.Tanh, scale=0.5)
+            else:
+                nc.scalar.activation(out=tanh_g[h][:], in_=og_raw[h][:], func=ACT.Tanh, scale=0.5)
+
+        def gate_v(h):
+            nc.vector.tensor_scalar(out=gate[h][:], in0=tanh_g[h][:], scalar1=0.5, scalar2=0.5, op0=ALU.mult, op1=ALU.add)
+
+        def gate_s(h):
+            nc.scalar.activation(out=gate[h][:], in_=tanh_g[h][:], func=ACT.Copy, scale=0.5, bias=0.5)
+
+        def interleave(h, u):
+            src = w_rows[h][:].rearrange("p (r c i) -> p c r i", r=PACK, i=4)
+            nc.vector.tensor_copy(out=w_bf[h][u][:].rearrange("p (c i r) -> p c r i", r=PACK, i=4),
+                                  in_=src[:, 64 * u:64 * (u + 1)])
+
+        def quantize(h, u):
+            nc.vector.quantize_mx(out=w_codes[h][u][:].bitcast(FP8X4), scales=w_scales[h][u][:], in_=w_bf[h][u][:])
+
+        def product(h):
+            feat = slice(T * (h % 2), T * (h % 2 + 1))
+            for c in range(PACK):
+                cols = slice(T * (c % 2), T * (c % 2 + 1))
+                nc.tensor.matmul_mx(out=y_bank[:, T * c:T * (c + 1)],
+                                    lhsT=w_codes[h][c // 2][:, cols].bitcast(FP8X4), lhsT_scale=w_scales[h][c // 2][:, cols],
+                                    rhs=v_codes[h // 2][:, feat].bitcast(FP8X4), rhs_scale=v_scales[h // 2][:, feat],
+                                    start=True, stop=True)
+
+        def recip(h):
+            nc.vector.reciprocal(out=rec[h][:], in_=y_bank[:].rearrange("p (c e) -> p c e", c=PACK)[:, :, T - 1])
+
+        def finish(h):
+            for u in range(2):
+                for cc in range(2):
+                    c = 2 * u + cc
+                    nc.vector.scalar_tensor_tensor(out=res[h][u][:, T * cc:T * (cc + 1)], in0=y_bank[:, T * c:T * (c + 1)],
+                                                   scalar=rec[h][:, c:c + 1], in1=gate[h][:, T * c:T * (c + 1)],
+                                                   op0=ALU.mult, op1=ALU.mult)
+                nc.sync.dma_start(out=out_rows[h, :, 2 * T * u:2 * T * (u + 1)], in_=res[h][u][:])
+
+        def middle(h, on_vector=True):
+            interleave(h, 0)
+            if h > 0:
+                if on_vector:
+                    gate_v(h - 1)
+                recip(h - 1)
+            interleave(h, 1)
+            if h > 0:
+                finish(h - 1)
+            quantize(h, 0)
+            quantize(h, 1)
+
+        A, B, C, E = 0, 1, 2, 3
+        scores(A, 0); scores(A, 1); scores(C, 0)
+        weights(A, 0); scores(A, 2)
+        weights(A, 1); scores(A, 3); scores(B, 0); scores(B, 1)
+        weights(C, 0); scores(C, 1)
+        weights(A, 2)
+        weights(A, 3)
+        middle(A)
+        weights(B, 0); scores(B, 2)
+        weights(B, 1); scores(B, 3)
+        weights(C, 1); scores(C, 2)
+        product(A)
+        weights(B, 2)
+        weights(B, 3)
+        tanh(0)
+        middle(B)
+        weights(C, 2); scores(C, 3); scores(E, 0); scores(E, 1)
+        product(B)
+        tanh(1)
+        weights(C, 3)
+        middle(C)
+        weights(E, 0); scores(E, 2)
+        weights(E, 1); scores(E, 3)
+        product(C)
+        tanh(2)
+        weights(E, 2)
+        weights(E, 3)
+        gate_s(2)
+        tanh(3)
+        middle(E, on_vector=False)
+        product(E)
+        gate_v(3)
+        recip(3)
+        finish(3)

@@ -19,8 +19,8 @@ ROWS = 32
 T = 128
 LN_LOW = 2.0 ** -63
 LN_HIGH = 2.0 ** 64
-Q_VECTOR = 84
-BANKS = (2, 2, 1, 2)
+Q_VECTOR = 24
+BANKS = (2, 2, 2, 1)
 
 
 def tile_rows_gate_kernel(tc, qT, kT, t, v, og, out):
@@ -40,18 +40,20 @@ def tile_rows_gate_kernel(tc, qT, kT, t, v, og, out):
         q_raw = sbuf("q_raw", PACK * NQ, F32)
         v_raw = [sbuf("v_raw%d" % h, PACK * T, F32) for h in range(H)]
         og_raw = [None] + [sbuf("og_raw%d" % h, PACK * T, F32) for h in range(1, H)]
-        og_rows = og.rearrange("h (m c) e -> h m (c e)", c=PACK)
-        out_rows = out.rearrange("h (m c) e -> h m (c e)", c=PACK)
+        og_rows = og.rearrange("h (u m c) e -> h m u (c e)", u=2, c=2)
+        out_rows = out.rearrange("h (u m c) e -> h m u (c e)", u=2, c=2)
 
         nc.sync.dma_start(out=t_raw[:], in_=t.rearrange("(p j) o -> p (j o)", j=PACK))
         nc.sync.dma_start(out=k_raw[:], in_=kT.rearrange("h (p j) n -> (h p) (j n)", j=PACK))
-        nc.scalar.dma_start(out=og_first[:], in_=og_rows[0, :, 0:T])
+        nc.scalar.dma_start(out=og_first[:], in_=og_rows[0, :, 0, 0:T])
         nc.sync.dma_start(out=q_raw[:], in_=qT.rearrange("h (p j) n -> (h p) (j n)", j=PACK))
+        nc.sync.dma_start(out=og_rest[:, 0:T], in_=og_rows[0, :, 0, T:])
+        nc.sync.dma_start(out=og_rest[:, T:], in_=og_rows[0, :, 1, :])
+        nc.sync.dma_start(out=og_raw[1][:].rearrange("p (u x) -> p u x", u=2), in_=og_rows[1])
         for h in range(H):
             nc.sync.dma_start(out=v_raw[h][:], in_=v[h].rearrange("(p j) e -> p (j e)", j=PACK))
-        nc.sync.dma_start(out=og_rest[:], in_=og_rows[0, :, T:])
-        for h in range(1, H):
-            nc.sync.dma_start(out=og_raw[h][:], in_=og_rows[h])
+        for h in range(2, H):
+            nc.sync.dma_start(out=og_raw[h][:].rearrange("p (u x) -> p u x", u=2), in_=og_rows[h])
 
         t_abs = sbuf("t_abs", PACK, F32)
         t_sign = sbuf("t_sign", PACK, F32)
@@ -73,7 +75,7 @@ def tile_rows_gate_kernel(tc, qT, kT, t, v, og, out):
         nc.scalar.activation(out=tanh_g[0][:, 0:T], in_=og_first[:], func=ACT.Tanh, scale=0.5)
 
         k_bf = sbuf("k_bf", PACK * N, BF16)
-        q_bf = sbuf("q_bf", PACK * NQ, BF16)
+        q_bf = [sbuf("q_bf%d" % u, 2 * NQ, BF16) for u in range(2)]
         k_codes = sbuf("k_codes", N, U32)
         k_scales = sbuf("k_scales", N, U8)
         q_codes = [sbuf("q_codes%d" % u, NQ // 2, U32) for u in range(2)]
@@ -87,23 +89,26 @@ def tile_rows_gate_kernel(tc, qT, kT, t, v, og, out):
         nc.vector.tensor_copy(out=k_dst, in_=k_src)
         nc.vector.tensor_tensor(out=ln_t[:], in0=ln_parts[:, 0:PACK], in1=ln_parts[:, PACK:], op=ALU.add)
         nc.vector.quantize_mx(out=k_codes[:].bitcast(FP8X4), scales=k_scales[:], in_=k_bf[:])
-        q_dst, q_src = dealt(q_bf, q_raw)
-        nc.vector.tensor_copy(out=q_dst[:, 0:Q_VECTOR], in_=q_src[:, 0:Q_VECTOR])
-        nc.scalar.copy(out=q_dst[:, Q_VECTOR:], in_=q_src[:, Q_VECTOR:])
+        q_src = q_raw[:].rearrange("p (j u n i c) -> p u n j i c", j=PACK, u=2, i=2, c=2)
+        q_dst = [q_bf[u][:].rearrange("p (c n i j) -> p n j i c", j=PACK, i=2, c=2) for u in range(2)]
+        nc.vector.tensor_copy(out=q_dst[0], in_=q_src[:, 0])
+        nc.vector.tensor_copy(out=q_dst[1][:, 0:Q_VECTOR], in_=q_src[:, 1, 0:Q_VECTOR])
+        nc.scalar.copy(out=q_dst[1][:, Q_VECTOR:], in_=q_src[:, 1, Q_VECTOR:])
         for u in range(2):
-            nc.vector.quantize_mx(out=q_codes[u][:].bitcast(FP8X4), scales=q_scales[u][:],
-                                  in_=q_bf[:, u * 2 * NQ:(u + 1) * 2 * NQ])
+            nc.vector.quantize_mx(out=q_codes[u][:].bitcast(FP8X4), scales=q_scales[u][:], in_=q_bf[u][:])
 
         v_bf = [sbuf("v_bf%d" % g, 2 * PACK * T, BF16) for g in range(2)]
         v_codes = [sbuf("v_codes%d" % g, 2 * T, U32) for g in range(2)]
         v_scales = [sbuf("v_scales%d" % g, 2 * T, U8) for g in range(2)]
         sign_b = t_sign[:, 0:PACK].unsqueeze(1).unsqueeze(3).to_broadcast([P, T // 4, PACK, 4])
-        for h in range(H):
+
+        def values(h):
             dst = v_bf[h // 2][:, (h % 2) * PACK * T:(h % 2 + 1) * PACK * T]
             nc.vector.tensor_tensor(out=dst.rearrange("p (c i j) -> p c j i", i=4, j=PACK),
                                     in0=v_raw[h][:].rearrange("p (j c i) -> p c j i", i=4, j=PACK),
                                     in1=sign_b, op=ALU.mult)
-        for g in range(2):
+
+        def values_quantize(g):
             nc.vector.quantize_mx(out=v_codes[g][:].bitcast(FP8X4), scales=v_scales[g][:], in_=v_bf[g][:])
 
         banks = [[ps.tile([P, NQ], F32, name="score%d_%d" % (h, b)) for b in range(BANKS[h])] for h in range(H)]
@@ -142,10 +147,9 @@ def tile_rows_gate_kernel(tc, qT, kT, t, v, og, out):
         def gate_s(h):
             nc.scalar.activation(out=gate[h][:], in_=tanh_g[h][:], func=ACT.Copy, scale=0.5, bias=0.5)
 
-        def interleave(h, u):
+        def interleave(h, u, copy=nc.vector.tensor_copy):
             src = w_rows[h][:].rearrange("p (r c i) -> p c r i", r=PACK, i=4)
-            nc.vector.tensor_copy(out=w_bf[h][u][:].rearrange("p (c i r) -> p c r i", r=PACK, i=4),
-                                  in_=src[:, 64 * u:64 * (u + 1)])
+            copy(out=w_bf[h][u][:].rearrange("p (c i r) -> p c r i", r=PACK, i=4), in_=src[:, 64 * u:64 * (u + 1)])
 
         def quantize(h, u):
             nc.vector.quantize_mx(out=w_codes[h][u][:].bitcast(FP8X4), scales=w_scales[h][u][:], in_=w_bf[h][u][:])
@@ -169,13 +173,11 @@ def tile_rows_gate_kernel(tc, qT, kT, t, v, og, out):
                     nc.vector.scalar_tensor_tensor(out=res[h][u][:, T * cc:T * (cc + 1)], in0=y_bank[:, T * c:T * (c + 1)],
                                                    scalar=rec[h][:, c:c + 1], in1=gate[h][:, T * c:T * (c + 1)],
                                                    op0=ALU.mult, op1=ALU.mult)
-                nc.sync.dma_start(out=out_rows[h, :, 2 * T * u:2 * T * (u + 1)], in_=res[h][u][:])
+                nc.sync.dma_start(out=out_rows[h, :, u, :], in_=res[h][u][:])
 
-        def middle(h, on_vector=True):
+        def middle(h):
             interleave(h, 0)
             if h > 0:
-                if on_vector:
-                    gate_v(h - 1)
                 recip(h - 1)
             interleave(h, 1)
             if h > 0:
@@ -184,36 +186,31 @@ def tile_rows_gate_kernel(tc, qT, kT, t, v, og, out):
             quantize(h, 1)
 
         A, B, C, E = 0, 1, 2, 3
-        scores(A, 0); scores(A, 1); scores(C, 0)
+        tanh(A); tanh(B)
+        values(0); values(1); values(2); values_quantize(0); values(3); gate_v(A); values_quantize(1); gate_v(B)
+        scores(A, 0); scores(A, 1); scores(B, 0)
         weights(A, 0); scores(A, 2)
-        weights(A, 1); scores(A, 3); scores(B, 0); scores(B, 1)
-        weights(C, 0); scores(C, 1)
+        weights(A, 1); scores(A, 3); scores(B, 1); scores(E, 0)
+        weights(B, 0); scores(B, 2)
         weights(A, 2)
         weights(A, 3)
         middle(A)
-        weights(B, 0); scores(B, 2)
-        weights(B, 1); scores(B, 3)
-        weights(C, 1); scores(C, 2)
-        product(A)
+        weights(B, 1); scores(B, 3); scores(C, 0); scores(C, 1)
+        weights(E, 0); product(A); scores(E, 1)
         weights(B, 2)
         weights(B, 3)
-        tanh(0)
         middle(B)
-        weights(C, 2); scores(C, 3); scores(E, 0); scores(E, 1)
-        product(B)
-        tanh(1)
+        weights(C, 0); scores(C, 2)
+        weights(C, 1); scores(C, 3)
+        weights(E, 1); scores(E, 2); product(B)
+        weights(C, 2)
         weights(C, 3)
         middle(C)
-        weights(E, 0); scores(E, 2)
-        weights(E, 1); scores(E, 3)
-        product(C)
-        tanh(2)
-        weights(E, 2)
-        weights(E, 3)
-        gate_s(2)
-        tanh(3)
-        middle(E, on_vector=False)
+        weights(E, 2); scores(E, 3)
+        tanh(C); gate_s(C)
+        weights(E, 3); product(C)
+        interleave(E, 1, nc.scalar.copy)
+        tanh(E)
+        interleave(E, 0); recip(C); quantize(E, 0); finish(C); quantize(E, 1)
         product(E)
-        gate_v(3)
-        recip(3)
-        finish(3)
+        gate_v(E); recip(E); finish(E)

@@ -20,6 +20,8 @@ T = 128
 LN_LOW = 2.0 ** -63
 LN_HIGH = 2.0 ** 64
 Q_VECTOR = 24
+K_VECTOR = 92
+FIRST = 32
 BANKS = (2, 2, 2, 1)
 
 
@@ -34,8 +36,8 @@ def tile_rows_gate_kernel(tc, qT, kT, t, v, og, out):
             return sb.tile([P, width], dtype, name=name, align_bytes=64)
 
         t_raw = sbuf("t_raw", PACK, F32)
-        og_first = sbuf("og_first", T, F32)
-        og_rest = sbuf("og_rest", 3 * T, F32)
+        og_first = sbuf("og_first", FIRST, F32)
+        og_rest = sbuf("og_rest", PACK * T - FIRST, F32)
         k_raw = sbuf("k_raw", PACK * N, F32)
         q_raw = sbuf("q_raw", PACK * NQ, F32)
         v_raw = [sbuf("v_raw%d" % h, PACK * T, F32) for h in range(H)]
@@ -45,10 +47,10 @@ def tile_rows_gate_kernel(tc, qT, kT, t, v, og, out):
 
         nc.sync.dma_start(out=t_raw[:], in_=t.rearrange("(p j) o -> p (j o)", j=PACK))
         nc.sync.dma_start(out=k_raw[:], in_=kT.rearrange("h (p j) n -> (h p) (j n)", j=PACK))
-        nc.scalar.dma_start(out=og_first[:], in_=og_rows[0, :, 0, 0:T])
+        nc.scalar.dma_start(out=og_first[:], in_=og_rows[0, :, 0, 0:FIRST])
         nc.sync.dma_start(out=q_raw[:], in_=qT.rearrange("h (p j) n -> (h p) (j n)", j=PACK))
-        nc.sync.dma_start(out=og_rest[:, 0:T], in_=og_rows[0, :, 0, T:])
-        nc.sync.dma_start(out=og_rest[:, T:], in_=og_rows[0, :, 1, :])
+        nc.sync.dma_start(out=og_rest[:, 0:2 * T - FIRST], in_=og_rows[0, :, 0, FIRST:])
+        nc.sync.dma_start(out=og_rest[:, 2 * T - FIRST:], in_=og_rows[0, :, 1, :])
         nc.sync.dma_start(out=og_raw[1][:].rearrange("p (u x) -> p u x", u=2), in_=og_rows[1])
         for h in range(H):
             nc.sync.dma_start(out=v_raw[h][:], in_=v[h].rearrange("(p j) e -> p (j e)", j=PACK))
@@ -58,21 +60,22 @@ def tile_rows_gate_kernel(tc, qT, kT, t, v, og, out):
         t_abs = sbuf("t_abs", PACK, F32)
         t_sign = sbuf("t_sign", PACK, F32)
         t_step = sbuf("t_step", PACK, F32)
-        t_inv = sbuf("t_inv", PACK, F32)
-        t_parts = sbuf("t_parts", 2 * PACK, F32)
-        ln_parts = sbuf("ln_parts", 2 * PACK, F32)
+        t_parts = sbuf("t_parts", 3 * PACK, F32)
+        ln_parts = sbuf("ln_parts", 3 * PACK, F32)
         ln_t = sbuf("ln_t", PACK, F32)
         nc.vector.scalar_tensor_tensor(out=t_abs[:], in0=t_raw[:], scalar=-1.0, in1=t_raw[:], op0=ALU.mult, op1=ALU.max)
         nc.vector.tensor_scalar(out=t_step[:], in0=t_raw[:], scalar1=0.0, scalar2=2.0, op0=ALU.is_ge, op1=ALU.mult)
         nc.vector.tensor_scalar(out=t_parts[:, 0:PACK], in0=t_abs[:], scalar1=LN_LOW, scalar2=LN_HIGH, op0=ALU.max, op1=ALU.min)
+        nc.vector.tensor_scalar(out=t_parts[:, PACK:2 * PACK], in0=t_abs[:], scalar1=1.0 / LN_HIGH, scalar2=1.0, op0=ALU.mult, op1=ALU.max)
+        nc.vector.tensor_scalar(out=t_parts[:, 2 * PACK:], in0=t_abs[:], scalar1=LN_LOW, scalar2=1.0 / LN_LOW, op0=ALU.min, op1=ALU.mult)
         nc.vector.tensor_scalar(out=t_sign[:], in0=t_step[:], scalar1=-1.0, scalar2=None, op0=ALU.add)
-        nc.vector.reciprocal(out=t_inv[:], in_=t_parts[:, 0:PACK])
-        nc.vector.tensor_tensor(out=t_parts[:, PACK:], in0=t_abs[:], in1=t_inv[:], op=ALU.mult)
         nc.scalar.activation(out=ln_parts[:], in_=t_parts[:], func=ACT.Ln)
+        nc.vector.tensor_reduce(out=ln_t[:], in_=ln_parts[:].rearrange("p (s j) -> p j s", j=PACK),
+                                axis=mybir.AxisListType.X, op=ALU.add)
 
         gate = [sbuf("gate%d" % h, PACK * T, F32) for h in range(H)]
         tanh_g = [sbuf("tanh_g%d" % h, PACK * T, F32) for h in range(H)]
-        nc.scalar.activation(out=tanh_g[0][:, 0:T], in_=og_first[:], func=ACT.Tanh, scale=0.5)
+        nc.scalar.activation(out=tanh_g[0][:, 0:FIRST], in_=og_first[:], func=ACT.Tanh, scale=0.5)
 
         k_bf = sbuf("k_bf", PACK * N, BF16)
         q_bf = [sbuf("q_bf%d" % u, 2 * NQ, BF16) for u in range(2)]
@@ -86,8 +89,8 @@ def tile_rows_gate_kernel(tc, qT, kT, t, v, og, out):
                     raw[:].rearrange("p (j m c) -> p m j c", c=PACK, j=PACK))
 
         k_dst, k_src = dealt(k_bf, k_raw)
-        nc.vector.tensor_copy(out=k_dst, in_=k_src)
-        nc.vector.tensor_tensor(out=ln_t[:], in0=ln_parts[:, 0:PACK], in1=ln_parts[:, PACK:], op=ALU.add)
+        nc.vector.tensor_copy(out=k_dst[:, 0:K_VECTOR], in_=k_src[:, 0:K_VECTOR])
+        nc.scalar.copy(out=k_dst[:, K_VECTOR:], in_=k_src[:, K_VECTOR:])
         nc.vector.quantize_mx(out=k_codes[:].bitcast(FP8X4), scales=k_scales[:], in_=k_bf[:])
         q_src = q_raw[:].rearrange("p (j u n i c) -> p u n j i c", j=PACK, u=2, i=2, c=2)
         q_dst = [q_bf[u][:].rearrange("p (c n i j) -> p n j i c", j=PACK, i=2, c=2) for u in range(2)]
@@ -120,16 +123,16 @@ def tile_rows_gate_kernel(tc, qT, kT, t, v, og, out):
         rec = [sbuf("rec%d" % h, PACK, F32) for h in range(H)]
         res = [[sbuf("res%d_%d" % (h, u), 2 * T, F32) for u in range(2)] for h in range(H)]
 
-        def scores(h, r):
-            bank = banks[h][r % BANKS[h]]
-            rows = slice(ROWS * h, ROWS * (h + 1))
-            keys = slice(T * r, T * (r + 1))
+        def scores(*groups):
             for c in range(PACK):
                 cols = slice(T * (c % 2), T * (c % 2 + 1))
-                nc.tensor.matmul_mx(out=bank[:, T * c:T * (c + 1)],
-                                    lhsT=k_codes[rows, keys].bitcast(FP8X4), lhsT_scale=k_scales[rows, keys],
-                                    rhs=q_codes[c // 2][rows, cols].bitcast(FP8X4), rhs_scale=q_scales[c // 2][rows, cols],
-                                    start=True, stop=True)
+                for h, r in groups:
+                    rows = slice(ROWS * h, ROWS * (h + 1))
+                    keys = slice(T * r, T * (r + 1))
+                    nc.tensor.matmul_mx(out=banks[h][r % BANKS[h]][:, T * c:T * (c + 1)],
+                                        lhsT=k_codes[rows, keys].bitcast(FP8X4), lhsT_scale=k_scales[rows, keys],
+                                        rhs=q_codes[c // 2][rows, cols].bitcast(FP8X4),
+                                        rhs_scale=q_scales[c // 2][rows, cols], start=True, stop=True)
 
         def weights(h, r):
             nc.scalar.activation(out=w_rows[h][:, NQ * r:NQ * (r + 1)], in_=banks[h][r % BANKS[h]][:],
@@ -137,7 +140,7 @@ def tile_rows_gate_kernel(tc, qT, kT, t, v, og, out):
 
         def tanh(h):
             if h == 0:
-                nc.scalar.activation(out=tanh_g[0][:, T:], in_=og_rest[:], func=ACT.Tanh, scale=0.5)
+                nc.scalar.activation(out=tanh_g[0][:, FIRST:], in_=og_rest[:], func=ACT.Tanh, scale=0.5)
             else:
                 nc.scalar.activation(out=tanh_g[h][:], in_=og_raw[h][:], func=ACT.Tanh, scale=0.5)
 
@@ -177,36 +180,36 @@ def tile_rows_gate_kernel(tc, qT, kT, t, v, og, out):
 
         def middle(h):
             interleave(h, 0)
-            if h > 0:
-                recip(h - 1)
             interleave(h, 1)
             if h > 0:
-                finish(h - 1)
+                recip(h - 1)
             quantize(h, 0)
+            if h > 0:
+                finish(h - 1)
             quantize(h, 1)
 
         A, B, C, E = 0, 1, 2, 3
         tanh(A); tanh(B)
         values(0); values(1); values(2); values_quantize(0); values(3); gate_v(A); values_quantize(1); gate_v(B)
-        scores(A, 0); scores(A, 1); scores(B, 0)
-        weights(A, 0); scores(A, 2)
-        weights(A, 1); scores(A, 3); scores(B, 1); scores(E, 0)
-        weights(B, 0); scores(B, 2)
+        scores((A, 0)); scores((A, 1)); scores((B, 0))
+        weights(A, 0); scores((A, 2))
+        weights(A, 1); scores((A, 3)); scores((B, 1)); scores((E, 0), (C, 0))
+        weights(B, 0); scores((B, 2))
         weights(A, 2)
         weights(A, 3)
         middle(A)
-        weights(B, 1); scores(B, 3); scores(C, 0); scores(C, 1)
-        weights(E, 0); product(A); scores(E, 1)
+        weights(B, 1); scores((B, 3))
+        weights(E, 0); scores((C, 1), (E, 1)); product(A)
         weights(B, 2)
         weights(B, 3)
         middle(B)
-        weights(C, 0); scores(C, 2)
-        weights(C, 1); scores(C, 3)
-        weights(E, 1); scores(E, 2); product(B)
+        weights(C, 0); scores((C, 2))
+        weights(C, 1); scores((C, 3))
+        weights(E, 1); scores((E, 2)); product(B)
         weights(C, 2)
         weights(C, 3)
         middle(C)
-        weights(E, 2); scores(E, 3)
+        weights(E, 2); scores((E, 3))
         tanh(C); gate_s(C)
         weights(E, 3); product(C)
         interleave(E, 1, nc.scalar.copy)

from contextlib import ExitStack

import concourse.mybir as mybir

H, D, NQ, N = 4, 128, 512, 512
FLOPS = 2 * 2 * H * NQ * N * D

F32 = mybir.dt.float32
BF16 = mybir.dt.bfloat16
U32 = mybir.dt.uint32
U8 = mybir.dt.uint8
FP8X4 = mybir.dt.float8_e4m3fn_x4
ALU = mybir.AluOpType
ACT = mybir.ActivationFunctionType

P = 128
PACK = 4
ROWS = 32
T = 128
LN_LOW = 2.0 ** -63
LN_HIGH = 2.0 ** 64
Q_VECTOR = 24
K_VECTOR = 92
FIRST = 32
BANKS = (2, 2, 2, 1)


def tile_rows_gate_kernel(tc, qT, kT, t, v, og, out):
    nc = tc.nc
    with ExitStack() as ctx:
        sb = ctx.enter_context(tc.tile_pool(name="sb", bufs=1))
        ps = ctx.enter_context(tc.psum_pool(name="ps", bufs=1))
        ctx.enter_context(tc.manual_schedule())

        def sbuf(name, width, dtype):
            return sb.tile([P, width], dtype, name=name, align_bytes=64)

        t_raw = sbuf("t_raw", PACK, F32)
        og_first = sbuf("og_first", FIRST, F32)
        og_rest = sbuf("og_rest", PACK * T - FIRST, F32)
        k_raw = sbuf("k_raw", PACK * N, F32)
        q_raw = sbuf("q_raw", PACK * NQ, F32)
        v_raw = [sbuf("v_raw%d" % h, PACK * T, F32) for h in range(H)]
        og_raw = [None] + [sbuf("og_raw%d" % h, PACK * T, F32) for h in range(1, H)]
        og_rows = og.rearrange("h (u m c) e -> h m u (c e)", u=2, c=2)
        out_rows = out.rearrange("h (u m c) e -> h m u (c e)", u=2, c=2)

        nc.sync.dma_start(out=t_raw[:], in_=t.rearrange("(p j) o -> p (j o)", j=PACK))
        nc.sync.dma_start(out=k_raw[:], in_=kT.rearrange("h (p j) n -> (h p) (j n)", j=PACK))
        nc.scalar.dma_start(out=og_first[:], in_=og_rows[0, :, 0, 0:FIRST])
        nc.sync.dma_start(out=q_raw[:], in_=qT.rearrange("h (p j) n -> (h p) (j n)", j=PACK))
        nc.sync.dma_start(out=og_rest[:, 0:2 * T - FIRST], in_=og_rows[0, :, 0, FIRST:])
        nc.sync.dma_start(out=og_rest[:, 2 * T - FIRST:], in_=og_rows[0, :, 1, :])
        nc.sync.dma_start(out=og_raw[1][:].rearrange("p (u x) -> p u x", u=2), in_=og_rows[1])
        for h in range(H):
            nc.sync.dma_start(out=v_raw[h][:], in_=v[h].rearrange("(p j) e -> p (j e)", j=PACK))
        for h in range(2, H):
            nc.sync.dma_start(out=og_raw[h][:].rearrange("p (u x) -> p u x", u=2), in_=og_rows[h])

        t_abs = sbuf("t_abs", PACK, F32)
        t_sign = sbuf("t_sign", PACK, F32)
        t_step = sbuf("t_step", PACK, F32)
        t_parts = sbuf("t_parts", 3 * PACK, F32)
        ln_parts = sbuf("ln_parts", 3 * PACK, F32)
        ln_t = sbuf("ln_t", PACK, F32)
        nc.vector.scalar_tensor_tensor(out=t_abs[:], in0=t_raw[:], scalar=-1.0, in1=t_raw[:], op0=ALU.mult, op1=ALU.max)
        nc.vector.tensor_scalar(out=t_step[:], in0=t_raw[:], scalar1=0.0, scalar2=2.0, op0=ALU.is_ge, op1=ALU.mult)
        nc.vector.tensor_scalar(out=t_parts[:, 0:PACK], in0=t_abs[:], scalar1=LN_LOW, scalar2=LN_HIGH, op0=ALU.max, op1=ALU.min)
        nc.vector.tensor_scalar(out=t_parts[:, PACK:2 * PACK], in0=t_abs[:], scalar1=1.0 / LN_HIGH, scalar2=1.0, op0=ALU.mult, op1=ALU.max)
        nc.vector.tensor_scalar(out=t_parts[:, 2 * PACK:], in0=t_abs[:], scalar1=LN_LOW, scalar2=1.0 / LN_LOW, op0=ALU.min, op1=ALU.mult)
        nc.vector.tensor_scalar(out=t_sign[:], in0=t_step[:], scalar1=-1.0, scalar2=None, op0=ALU.add)
        nc.scalar.activation(out=ln_parts[:], in_=t_parts[:], func=ACT.Ln)
        nc.vector.tensor_reduce(out=ln_t[:], in_=ln_parts[:].rearrange("p (s j) -> p j s", j=PACK),
                                axis=mybir.AxisListType.X, op=ALU.add)

        gate = [sbuf("gate%d" % h, PACK * T, F32) for h in range(H)]
        tanh_g = [sbuf("tanh_g%d" % h, PACK * T, F32) for h in range(H)]
        nc.scalar.activation(out=tanh_g[0][:, 0:FIRST], in_=og_first[:], func=ACT.Tanh, scale=0.5)

        k_bf = sbuf("k_bf", PACK * N, BF16)
        q_bf = [sbuf("q_bf%d" % u, 2 * NQ, BF16) for u in range(2)]
        k_codes = sbuf("k_codes", N, U32)
        k_scales = sbuf("k_scales", N, U8)
        q_codes = [sbuf("q_codes%d" % u, NQ // 2, U32) for u in range(2)]
        q_scales = [sbuf("q_scales%d" % u, NQ // 2, U8) for u in range(2)]

        def dealt(bf, raw):
            return (bf[:].rearrange("p (c m j) -> p m j c", c=PACK, j=PACK),
                    raw[:].rearrange("p (j m c) -> p m j c", c=PACK, j=PACK))

        k_dst, k_src = dealt(k_bf, k_raw)
        nc.vector.tensor_copy(out=k_dst[:, 0:K_VECTOR], in_=k_src[:, 0:K_VECTOR])
        nc.scalar.copy(out=k_dst[:, K_VECTOR:], in_=k_src[:, K_VECTOR:])
        nc.vector.quantize_mx(out=k_codes[:].bitcast(FP8X4), scales=k_scales[:], in_=k_bf[:])
        q_src = q_raw[:].rearrange("p (j u n i c) -> p u n j i c", j=PACK, u=2, i=2, c=2)
        q_dst = [q_bf[u][:].rearrange("p (c n i j) -> p n j i c", j=PACK, i=2, c=2) for u in range(2)]
        nc.vector.tensor_copy(out=q_dst[0], in_=q_src[:, 0])
        nc.vector.tensor_copy(out=q_dst[1][:, 0:Q_VECTOR], in_=q_src[:, 1, 0:Q_VECTOR])
        nc.scalar.copy(out=q_dst[1][:, Q_VECTOR:], in_=q_src[:, 1, Q_VECTOR:])
        for u in range(2):
            nc.vector.quantize_mx(out=q_codes[u][:].bitcast(FP8X4), scales=q_scales[u][:], in_=q_bf[u][:])

        v_bf = [sbuf("v_bf%d" % g, 2 * PACK * T, BF16) for g in range(2)]
        v_codes = [sbuf("v_codes%d" % g, 2 * T, U32) for g in range(2)]
        v_scales = [sbuf("v_scales%d" % g, 2 * T, U8) for g in range(2)]
        sign_b = t_sign[:, 0:PACK].unsqueeze(1).unsqueeze(3).to_broadcast([P, T // 4, PACK, 4])

        def values(h):
            dst = v_bf[h // 2][:, (h % 2) * PACK * T:(h % 2 + 1) * PACK * T]
            nc.vector.tensor_tensor(out=dst.rearrange("p (c i j) -> p c j i", i=4, j=PACK),
                                    in0=v_raw[h][:].rearrange("p (j c i) -> p c j i", i=4, j=PACK),
                                    in1=sign_b, op=ALU.mult)

        def values_quantize(g):
            nc.vector.quantize_mx(out=v_codes[g][:].bitcast(FP8X4), scales=v_scales[g][:], in_=v_bf[g][:])

        banks = [[ps.tile([P, NQ], F32, name="score%d_%d" % (h, b)) for b in range(BANKS[h])] for h in range(H)]
        y_bank = ps.tile([P, PACK * T], F32, name="y_bank")
        w_rows = [sbuf("w_rows%d" % h, PACK * NQ, BF16) for h in range(H)]
        w_bf = [[sbuf("w_bf%d_%d" % (h, u), 2 * NQ, BF16) for u in range(2)] for h in range(H)]
        w_codes = [[sbuf("w_codes%d_%d" % (h, u), NQ // 2, U32) for u in range(2)] for h in range(H)]
        w_scales = [[sbuf("w_scales%d_%d" % (h, u), NQ // 2, U8) for u in range(2)] for h in range(H)]
        rec = [sbuf("rec%d" % h, PACK, F32) for h in range(H)]
        res = [[sbuf("res%d_%d" % (h, u), 2 * T, F32) for u in range(2)] for h in range(H)]

        def scores(*groups):
            for c in range(PACK):
                cols = slice(T * (c % 2), T * (c % 2 + 1))
                for h, r in groups:
                    rows = slice(ROWS * h, ROWS * (h + 1))
                    keys = slice(T * r, T * (r + 1))
                    nc.tensor.matmul_mx(out=banks[h][r % BANKS[h]][:, T * c:T * (c + 1)],
                                        lhsT=k_codes[rows, keys].bitcast(FP8X4), lhsT_scale=k_scales[rows, keys],
                                        rhs=q_codes[c // 2][rows, cols].bitcast(FP8X4),
                                        rhs_scale=q_scales[c // 2][rows, cols], start=True, stop=True)

        def weights(h, r):
            nc.scalar.activation(out=w_rows[h][:, NQ * r:NQ * (r + 1)], in_=banks[h][r % BANKS[h]][:],
                                 func=ACT.Exp, bias=ln_t[:, r:r + 1])

        def tanh(h):
            if h == 0:
                nc.scalar.activation(out=tanh_g[0][:, FIRST:], in_=og_rest[:], func=ACT.Tanh, scale=0.5)
            else:
                nc.scalar.activation(out=tanh_g[h][:], in_=og_raw[h][:], func=ACT.Tanh, scale=0.5)

        def gate_v(h):
            nc.vector.tensor_scalar(out=gate[h][:], in0=tanh_g[h][:], scalar1=0.5, scalar2=0.5, op0=ALU.mult, op1=ALU.add)

        def gate_s(h):
            nc.scalar.activation(out=gate[h][:], in_=tanh_g[h][:], func=ACT.Copy, scale=0.5, bias=0.5)

        def interleave(h, u, copy=nc.vector.tensor_copy):
            src = w_rows[h][:].rearrange("p (r c i) -> p c r i", r=PACK, i=4)
            copy(out=w_bf[h][u][:].rearrange("p (c i r) -> p c r i", r=PACK, i=4), in_=src[:, 64 * u:64 * (u + 1)])

        def quantize(h, u):
            nc.vector.quantize_mx(out=w_codes[h][u][:].bitcast(FP8X4), scales=w_scales[h][u][:], in_=w_bf[h][u][:])

        def product(h):
            feat = slice(T * (h % 2), T * (h % 2 + 1))
            for c in range(PACK):
                cols = slice(T * (c % 2), T * (c % 2 + 1))
                nc.tensor.matmul_mx(out=y_bank[:, T * c:T * (c + 1)],
                                    lhsT=w_codes[h][c // 2][:, cols].bitcast(FP8X4), lhsT_scale=w_scales[h][c // 2][:, cols],
                                    rhs=v_codes[h // 2][:, feat].bitcast(FP8X4), rhs_scale=v_scales[h // 2][:, feat],
                                    start=True, stop=True)

        def recip(h):
            nc.vector.reciprocal(out=rec[h][:], in_=y_bank[:].rearrange("p (c e) -> p c e", c=PACK)[:, :, T - 1])

        def finish(h):
            for u in range(2):
                for cc in range(2):
                    c = 2 * u + cc
                    nc.vector.scalar_tensor_tensor(out=res[h][u][:, T * cc:T * (cc + 1)], in0=y_bank[:, T * c:T * (c + 1)],
                                                   scalar=rec[h][:, c:c + 1], in1=gate[h][:, T * c:T * (c + 1)],
                                                   op0=ALU.mult, op1=ALU.mult)
                nc.sync.dma_start(out=out_rows[h, :, u, :], in_=res[h][u][:])

        def middle(h):
            interleave(h, 0)
            interleave(h, 1)
            if h > 0:
                recip(h - 1)
            quantize(h, 0)
            if h > 0:
                finish(h - 1)
            quantize(h, 1)

        A, B, C, E = 0, 1, 2, 3
        tanh(A); tanh(B)
        values(0); values(1); values(2); values_quantize(0); values(3); gate_v(A); values_quantize(1); gate_v(B)
        scores((A, 0)); scores((A, 1)); scores((B, 0))
        weights(A, 0); scores((A, 2))
        weights(A, 1); scores((A, 3)); scores((B, 1)); scores((E, 0), (C, 0))
        weights(B, 0); scores((B, 2))
        weights(A, 2)
        weights(A, 3)
        middle(A)
        weights(B, 1); scores((B, 3))
        weights(E, 0); scores((C, 1), (E, 1)); product(A)
        weights(B, 2)
        weights(B, 3)
        middle(B)
        weights(C, 0); scores((C, 2))
        weights(C, 1); scores((C, 3))
        weights(E, 1); scores((E, 2)); product(B)
        weights(C, 2)
        weights(C, 3)
        middle(C)
        weights(E, 2); scores((E, 3))
        tanh(C); gate_s(C)
        weights(E, 3); product(C)
        interleave(E, 1, nc.scalar.copy)
        tanh(E)
        interleave(E, 0); recip(C); quantize(E, 0); finish(C); quantize(E, 1)
        product(E)
        gate_v(E); recip(E); finish(E)
